import numpy as np, ml_dtypes
CORES = [66,74,82,90,194,202,210,218]
N = 8
import mx_ref
BF = ml_dtypes.bfloat16
def gcols(t, e):
    v = np.concatenate([t.reshape(8, 16, -1, 4), np.zeros((8, 16, 1, 4), BF)], axis=2)
    return np.ascontiguousarray(np.stack([v[g][:, e[g]] for g in range(8)])).reshape(128, -1)
def tile(rs):
    return np.stack(rs, axis=2).reshape(128, -1).astype(BF)
def pick(q, e):
    c = np.concatenate([q[0].reshape(128, -1, 4), np.zeros((128, 1, 4), np.uint8)], axis=1); s = np.concatenate([q[1], np.ones((16, 1), np.uint8)], axis=1)
    return (np.ascontiguousarray(c[:, e].reshape(128, -1)), np.ascontiguousarray(s[:, e]))
def join(*qs):
    return (np.concatenate([q[0] for q in qs], axis=1), np.concatenate([q[1] for q in qs], axis=1))
def put(q, e, v):
    c, s = q[0].reshape(128, -1, 4).copy(), q[1].copy(); c[:, e] = v[0].reshape(128, -1, 4); s[:, e] = v[1]
    return (c.reshape(128, -1), s)
def pk(c, s):
    return (np.ascontiguousarray(c), mx_ref.live(s))
def emit(q):
    return q[0], q[1]
def packed(v, rng):
    q = [mx_ref.quantize(np.ascontiguousarray(v[r])) for r in range(N)]
    return np.stack([a for a, b in q]), np.stack([mx_ref.plane(b, rng) for a, b in q])
def values_of_codes():
    e, c = np.zeros((128, 128, 4), np.float32), np.zeros((128, 2, 4), np.uint8)
    e[np.arange(128), np.arange(128), 0] = 1
    c[:127, :, 0] = np.arange(256).reshape(2, 128).T[:127]
    return mx_ref.matmul(mx_ref.quantize(e.reshape(128, 512).astype(BF)), (c.reshape(128, 8), np.full((16, 2), 127, np.uint8))).T.reshape(-1).astype(np.float64)
CODE_VALUE, SCALE_VALUE = values_of_codes(), 2.0 ** (np.arange(256) - 127.0)
def decode(q):
    return (CODE_VALUE[q[0]].reshape(16, 8, -1, 4) * SCALE_VALUE[q[1]][:, None, :, None] + 0.0).reshape(128, -1).astype(np.float32)
def f(rng, *shape):
    return mx_ref.flush((rng.standard_normal(shape, dtype=np.float32) * np.exp2(rng.integers(-2, 3, shape[:-1] + (1,)))).astype(BF))
def wide(rng, *shape, cols=0):
    v = rng.standard_normal(shape, dtype=np.float32) * np.exp2(rng.integers(-12, 13, shape)).astype(np.float32)
    if cols: v *= np.repeat(np.exp2(rng.integers(-cols, cols + 1, shape[:-2] + (1, shape[-1] // 4))) * (rng.random(shape[:-2] + (1, shape[-1] // 4)) > 0.0625), 4, axis=-1).astype(np.float32)
    return mx_ref.flush(v.astype(BF))
C, STEP = 224, [4, 1, 2]
def numbers_of(rng):
    return {"x": np.array(f(rng, N, 128, 4 * C)), "u": np.array(f(rng, N, 128, 512)), "v": np.array(f(rng, N, 128, 512))}
def layers(rng):
    return np.array(f(rng, N, 128, 2048)).reshape(N, 8, 16, 4, 8, 16, 4)
def weights(rng, w):
    c, p = packed(np.ascontiguousarray(w).reshape(N, 128, 2048), rng)
    return {"wc": c, "ws": p}
def both(x, u):
    return {"x": x.astype(np.float32).reshape(N, 128, 4 * C).astype(BF), "u": u.astype(np.float32).reshape(N, 128, 512).astype(BF)}
def setup_inputs(rng):
    return {**numbers_of(rng), **weights(rng, layers(rng))}
def setup_inputs_ties(rng):
    d = numbers_of(rng)
    e = rng.permutation(N)
    x = rng.integers(-1, 2, (N, 128, C, 4)) * (rng.random((N, 128, C, 4)) < 0.09375)
    u = rng.integers(-1, 2, (N, 128, 128, 4)) * (rng.random((N, 128, 128, 4)) < 0.09375)
    x[e[0]] = x[e[0]][:, :1].copy()
    x[e[1]] = 0
    u[e[2]] = u[e[2]][:, :1].copy()
    w = np.zeros((N, 128, 512, 4), np.float32)
    for r in range(N):
        a, c = rng.permutation(512)[:128], rng.permutation(512)[:128]
        w[r, a // 4, c, a % 4] = 64
    return {**both(x, u), "v": d["v"], **weights(rng, w.astype(BF))}
def setup_inputs_near(rng):
    d = numbers_of(rng)
    h, o = rng.permutation(8), rng.permutation(N) % 4
    x = d["x"].astype(np.float32).reshape(N, 8, 16, C, 4)
    u = d["u"].astype(np.float32).reshape(N, 8, 16, 128, 4)
    x[:, :, 8:] = 0
    u[:, :, :8] = 0
    x[:, h[:2], :8] = 0
    p = np.exp2(np.arange(4) - 23.0)
    for r in range(N):
        k = 1.0 if o[r] < 2 else 2.0 ** -29
        if o[r] == 3:
            x[r, h[0], 0, :, 0] = rng.choice([1.0, 1.125], C) * 2.0 ** -30
            u[r, h[0], 0, :, 0] = rng.choice([1.125, 1.25], 128) * 2.0 ** -30
        else:
            x[r, h[0], 0, :, 0] = -1.0 if o[r] == 1 else 1.0
            u[r, h[0], 0, :, 0] = k
            x[r, h[1], 0] = ((rng.integers(0, 16, (C, 1)) >> np.arange(4)) & 1) * p
            u[r, h[1], 0] = k
            x[r, h[1], 1] = p
            u[r, h[1], 1] = ((rng.integers(0, 16, (128, 1)) >> np.arange(4)) & 1) * k
            x[r, h[1], 2, :, 0] = 2.0 ** -10
            u[r, h[1], 2, :, 0] = k
        x[r, h[0], 0, rng.integers(C), 0] = 2.0 ** 29
    w = layers(rng)
    w[:, h[:2], :8] = 0
    for g in h[:2]: w[:, :, :, :, g, :8] = 0
    return {**both(x, u), "v": d["v"], **weights(rng, w)}
def setup_inputs_huge(rng):
    d = numbers_of(rng)
    e = rng.permutation(N)
    x = 0.7 + 0.3 * rng.random((N, 8, 16, C, 4))
    u = 0.7 + 0.3 * rng.random((N, 8, 16, 128, 4))
    for i in range(N):
        r = e[i]
        if i == 0:
            x[r] = -0.94 - 0.06 * rng.random((8, 16, C, 4))
            x[r][:, :, rng.permutation(C)[:4]] *= -1.0
            u[r] = 0.94 + 0.06 * rng.random((8, 16, 128, 4))
        elif i % 2 == 1: u[r] *= -1.0
        else:
            x[r] *= rng.choice([-1.0, 1.0], (1, 1, C, 1))
            u[r] *= rng.choice([-1.0, 1.0], (1, 1, 128, 1))
    w = np.zeros((N, 128, 4, 128, 4), np.float32)
    i = np.arange(128)
    for b in range(4): w[:, i, b, i, b] = -1
    return {**both(x * 2.0 ** 30, u * 2.0 ** 30), "v": d["v"], **weights(rng, w.astype(BF))}
def setup_inputs_odd(rng):
    d = numbers_of(rng)
    x = d["x"].astype(np.float32).reshape(N, 8, 16, C, 4)
    u = d["u"].astype(np.float32).reshape(N, 8, 16, 128, 4)
    for a, n in ((x, C), (u, 128)):
        a[:, :, :8] = (2 * rng.integers(0, 8, (N, 8, 8, n, 4)) + 1) * rng.choice([-1.0, 1.0], (N, 8, 8, n, 4)) * 2.0 ** -16
        a[:, :, 0, :, 0] = rng.choice([1.625, 1.75, 1.875, 1.96875], (N, 8, n))
        a[:, :, 8] = 0
        a[:, :, 8, :, 0] = 1
    w = layers(rng)
    w[:, :, :, :, :, :9] = 0
    for g in range(8): w[:, g, 8, 0, g, 0, 0] = 3
    return {**both(x, u), "v": d["v"], **weights(rng, w)}
def setup_inputs_spread(rng):
    d = setup_inputs(rng)
    d["x"] = wide(rng, N, 128, 4 * C, cols=6)
    return d
def check_inputs(d):
    b = []
    for k in ("x", "u", "v"):
        a = np.abs(d[k].astype(np.float32))
        if not (np.isfinite(a).all() and ((a == 0) | (a >= 2.0 ** -30) & (a <= 2.0 ** 30)).all()): b.append("a value of " + k)
    none, least, most = [emit(mx_ref.quantize(np.full((128, 16), k, np.float32).astype(BF)))[1][0, 0] for k in (0.0, 2.0 ** -30, 2.0 ** 30)]
    for r in range(N):
        if ((d["wc"][r] == 0x7F) | (d["wc"][r] == 0xFF)).any(): b.append("wc: a code that is no number")
        s = mx_ref.live(d["ws"][r])
        if ((s != none) & ((s < least) | (s > most))).any(): b.append("ws: a scale out of range")
    return b
def reference(x, u, v, wc, ws):
    lay = [pk(wc[r], ws[r]) for r in range(N)]
    now = [mx_ref.quantize(x[r]) for r in range(N)]
    stat = [mx_ref.quantize(u[r]) for r in range(N)]
    down, along = np.zeros((N, 8, C), np.int64), np.zeros((N, 8, 128), np.int64)
    for h in STEP:
        sent = []
        for r in range(N):
            own = decode(now[r])
            s = mx_ref.matmul(stat[r], now[r]) + np.float32(0.0)
            down[r] = np.argmax(s.reshape(8, 16, C), axis=1) + 16 * np.arange(8)[:, None]
            along[r] = np.argsort(-s, axis=1, kind="stable")[:, :8].T
            a = gcols(decode(stat[r]).astype(BF), down[r]).astype(np.float32)
            z = mx_ref.quantize(((own + a) * np.float32(0.5)).astype(BF))
            now[r] = mx_ref.quantize(tile([mx_ref.matmul(pick(lay[r], np.arange(128 * b, 128 * b + 128)), z) * np.float32(0.03125) + own[:, b::4] for b in range(4)]))
            sent.append(mx_ref.quantize(gcols(decode(now[r]).astype(BF), along[r])))
        stat = [sent[(r - h) % N] for r in range(N)]
    y, op = np.zeros((N, 128, C), np.float32), np.zeros((N, 8, C + 128), np.float32)
    oc, osc = np.zeros((N, 128, 4 * C), np.uint8), np.zeros((N, 16, C), np.uint8)
    uc, usc = np.zeros((N, 128, 512), np.uint8), np.zeros((N, 16, 128), np.uint8)
    for r in range(N):
        y[r] = mx_ref.matmul(mx_ref.quantize(v[r]), now[r])
        op[r, :, :C] = down[r]
        op[r, :, C:] = along[r]
        oc[r], osc[r] = emit(now[r])
        uc[r], usc[r] = emit(stat[r])
    return {"y": y, "op": op, "oc": oc, "osc": osc, "uc": uc, "usc": usc}

@@ -1,0 +1,349 @@
+import numpy as np
+from concourse.bass import DstId, RemoteDMATransfer
+from concourse.mybir import dt, AluOpType, AxisListType, ActivationFunctionType
+
+STEP = [4, 1, 2]
+C = 224
+BIG = 1.0e29
+PS = 232
+F8 = "float8_e4m3fn_x4"
+ALU = AluOpType
+ACT = ActivationFunctionType
+
+SCRATCH = {
+    "xin": ("sbuf", [128, 4 * C], "bfloat16"), "uin": ("sbuf", [128, 512], "bfloat16"), "vin": ("sbuf", [128, 512], "bfloat16"),
+    "wq": ("sbuf", [128, 512], F8), "wsc": ("sbuf", [128, 512], "uint8"),
+    "qu": ("sbuf", [128, 128], F8), "squ": ("sbuf", [128, 128], "uint8"),
+    "qvv": ("sbuf", [128, 128], F8), "sqvv": ("sbuf", [128, 128], "uint8"),
+    "c32": ("sbuf", [128, 516], "bfloat16"), "dd": ("sbuf", [128, 516], "bfloat16"),
+    "dde": ("sbuf", [128, 516], "bfloat16"), "ddo": ("sbuf", [128, 516], "bfloat16"),
+    "cf": ("sbuf", [128, 512], F8), "scf": ("sbuf", [128, 512], "uint8"),
+    "ce": ("sbuf", [128, 512], F8), "sce": ("sbuf", [128, 512], "uint8"),
+    "cd": ("sbuf", [128, 512], F8), "scd": ("sbuf", [128, 512], "uint8"),
+    "zt": ("sbuf", [128, 4 * C], "bfloat16"), "xt": ("sbuf", [128, 4 * C], "bfloat16"), "vt": ("sbuf", [128, 512], "bfloat16"),
+    "bigc": ("sbuf", [128, C], "float32"), "rst": ("sbuf", [128, 128], "float32"),
+    "mones": ("sbuf", [128, 256], "bfloat16"), "ones": ("sbuf", [128, C], "bfloat16"), "mone7": ("sbuf", [128, 8], "float32"),
+    "pa": ("sbuf", [128, 288], "float32"), "nr": ("sbuf", [128, 256], "bfloat16"), "ag": ("sbuf", [128, 256], "bfloat16"),
+    "kt": ("sbuf", [128, 256], "bfloat16"), "ot": ("sbuf", [128, 32], "bfloat16"), "ott": ("sbuf", [128, 32], "bfloat16"),
+    "lst": ("sbuf", [128, 32], "uint16"),
+    "pb": ("sbuf", [128, 8 * PS], "float32"), "eq": ("sbuf", [128, 8], "float32"), "ne": ("sbuf", [128, 8], "float32"),
+    "fb": ("sbuf", [128, 8 * C], "bfloat16"), "cb": ("sbuf", [128, 8 * C], "bfloat16"), "junk": ("sbuf", [128, 8 * C], "bfloat16"),
+    "nb": ("sbuf", [128, 32], "float32"), "nt": ("sbuf", [128, 32], "float32"),
+    "ot2": ("sbuf", [128, 32], "float32"), "ott2": ("sbuf", [128, 32], "float32"), "lst2": ("sbuf", [128, 16], "uint16"),
+    "ip": ("sbuf", [128, 2], "int32"), "t1": ("sbuf", [128, 2], "int32"), "t2": ("sbuf", [128, 2], "int32"), "t3": ("sbuf", [128, 2], "int32"),
+    "col": ("sbuf", [128, 8], "float32"),
+    "cz": ("sbuf", [128, 96], "float32"), "czt": ("sbuf", [128, 96], "float32"), "off": ("sbuf", [128, 8], "uint16"),
+    "kf": ("sbuf", [128, 64], "float32"), "kft": ("sbuf", [128, 64], "float32"), "kfo": ("sbuf", [128, 64], "float32"),
+    "yb": ("sbuf", [128, C], "float32"),
+    "ps": ("psum", [128, 4096], "float32"),
+}
+for _r in range(4):
+    SCRATCH["qx%d" % _r] = ("sbuf", [128, C], F8)
+    SCRATCH["sx%d" % _r] = ("sbuf", [128, C], "uint8")
+for _r in range(3):
+    SCRATCH["ue%d" % _r] = ("sbuf", [128, C], F8)
+    SCRATCH["se%d" % _r] = ("sbuf", [128, C], "uint8")
+    SCRATCH["uo%d" % _r] = ("sbuf", [128, C], F8)
+    SCRATCH["so%d" % _r] = ("sbuf", [128, C], "uint8")
+    SCRATCH["qz%d" % _r] = ("sbuf", [128, C], F8)
+    SCRATCH["sz%d" % _r] = ("sbuf", [128, C], "uint8")
+    SCRATCH["pk%d" % _r] = ("sbuf", [128, 256], F8)
+    SCRATCH["sk%d" % _r] = ("sbuf", [128, 256], "uint8")
+    SCRATCH["qv%d" % _r] = ("sbuf", [128, 128], F8)
+    SCRATCH["sv%d" % _r] = ("sbuf", [128, 128], "uint8")
+    SCRATCH["land%d" % (_r + 1)] = ("sbuf", [128, 128], F8)
+    SCRATCH["lsc%d" % (_r + 1)] = ("sbuf", [128, 128], "uint8")
+SEMAPHORES = ["vs", "ts", "sa", "gc0", "dk", "dn", "ldx", "ldu", "ldv", "ldw", "ldp", "loc", "arr1", "arr2", "arr3", "st"]
+
+
+def rank_program(g, core, T, topo):
+    rank = T.rank_of(core)
+    if rank is None:
+        return
+    queue = {"v": g.vector, "t": g.tensor, "a": g.scalar, "s": g.sync, "g": g}
+    csem = {"v": "vs", "t": "ts", "a": "sa", "g": "gc0"}
+    known = {q: {} for q in queue}
+    count = {s: 0 for s in SEMAPHORES}
+    clocks = {s: {} for s in SEMAPHORES}
+    regs = {}
+
+    def merge(a, b):
+        for s, n in b.items():
+            if a.get(s, 0) < n:
+                a[s] = n
+
+    def deps(q, reads, writes):
+        out = []
+        for w, items in ((False, reads), (True, writes)):
+            for name, lo, hi in items:
+                bank = name.startswith("bank")
+                for (l, h, ww, qq, tok) in regs.get(name, []):
+                    if l >= hi or h <= lo:
+                        continue
+                    if bank:
+                        if qq == q and (q == "t" or not (w or ww)):
+                            continue
+                    elif not (w or ww):
+                        continue
+                    out.append(tok)
+        return out
+
+    def need(q, toks):
+        best = {}
+        for tk in toks:
+            s, n, c = tk
+            if known[q].get(s, 0) < n and (s not in best or best[s][1] < n):
+                best[s] = tk
+        for s in list(best):
+            if any(o != s and best[o][2].get(s, 0) >= best[s][1] for o in best):
+                del best[s]
+        for s, tk in best.items():
+            queue[q].wait_ge(T.sem[s], tk[1])
+            merge(known[q], tk[2])
+
+    def note(q, tok, reads, writes):
+        for name, lo, hi in writes:
+            old = regs.get(name, [])
+            regs[name] = [e for e in old if not (lo <= e[0] and e[1] <= hi)] + [(lo, hi, True, q, tok)]
+        for name, lo, hi in reads:
+            regs.setdefault(name, []).append((lo, hi, False, q, tok))
+
+    def token(q, s, n):
+        count[s] += n
+        c = dict(known[q])
+        merge(c, clocks[s])
+        c[s] = count[s]
+        clocks[s] = c
+        return (s, count[s], c)
+
+    def run(q, reads, writes, fn):
+        need(q, deps(q, reads, writes))
+        fn().then_inc(T.sem[csem[q]], 1)
+        tok = token(q, csem[q], 1)
+        note(q, tok, reads, writes)
+        return tok
+
+    def dmas(s, jobs):
+        ds = [deps(q, r, w) for q, r, w, o, i in jobs]
+        toks = []
+        for (q, r, w, o, i), d in zip(jobs, ds):
+            need(q, d)
+            queue[q].dma_start(o, i).then_inc(T.sem[s], 16)
+            toks.append(token(q, s, 16))
+        for q, r, w, o, i in jobs:
+            note(q, toks[-1], r, w)
+        return toks[-1]
+
+    def R(name, lo=0, hi=None):
+        return (name, lo, 1 << 20 if hi is None else hi)
+
+    def bank(j, n):
+        return T.ps[:, 512 * j:512 * j + n]
+
+    def mm(j, n, a, sa, alo, b, sb, blo, start, stop):
+        run("t", [R(a, alo, alo + 128), R(sa, alo, alo + 128), R(b, blo, blo + n), R(sb, blo, blo + n)], [R("bank%d" % j)],
+            lambda: g.tensor.matmul_mx(bank(j, n), T[a][:, alo:alo + 128], T[sa][:, alo:alo + 128], T[b][:, blo:blo + n], T[sb][:, blo:blo + n], start, stop))
+
+    def vec(reads, writes, fn):
+        return run("v", reads, writes, fn)
+
+    def act(reads, writes, fn):
+        return run("a", reads, writes, fn)
+
+    def fill(name, view, c, lo=0, hi=None):
+        vec([], [R(name, lo, hi)], lambda: g.vector.memset(view, c))
+
+    def quant(q, s, lo, n, tile, tlo, names):
+        vec(names, [R(q, lo, lo + n), R(s, lo, lo + n)], lambda: g.vector.quantize_mx(T[q][:, lo:lo + n], T[s][:, lo:lo + n], T[tile][:, tlo:tlo + 4 * n]))
+
+    dmas("ldx", [("s", [], [R("xin")], T.xin[:], T.x[:])])
+    dmas("ldu", [("a", [], [R("uin")], T.uin[:], T.u[:])])
+    dmas("ldw", [("s", [], [R("wq")], T.wq[:].bitcast(dt.uint8), T.wc[:])])
+    dmas("ldp", [("a", [], [R("wsc")], T.wsc[:], T.ws[:])])
+    dmas("ldv", [("s", [], [R("vin")], T.vin[:], T.v[:])])
+
+    fill("c32", T.c32[:], 32.0)
+    run("g", [], [R("ip")], lambda: g.iota(T.ip[:, 0:1], [[0, 1]], 0, 1))
+    run("g", [R("c32")], [R("dd")], lambda: g.affine_select(T.dd[:], T.c32[:], [[1, 516]], ALU.is_equal, 0.0, -3, -4))
+    for blk, base, pat in ((0, 0, [[20, 2], [4, 4], [1, 2]]), (1, 2, [[20, 2], [4, 4], [1, 2]]), (2, 0, [[2, 2], [4, 4], [1, 2]])):
+        for h in range(2):
+            lo = 32 * blk + 16 * h
+            run("g", [], [R("cz", lo, lo + 16)], lambda: g.iota(T.cz[:, lo:lo + 16], pat, base, 0, allow_small_or_imprecise_dtypes=True))
+    fill("rst", T.rst[:], BIG)
+    fill("rst", T.rst[:, 0:128:16], -BIG)
+    fill("pa", T.pa[:, 0:288:144], -BIG, 0, 1)
+    fill("mones", T.mones[:], -1.0)
+    fill("bigc", T.bigc[:], BIG)
+    fill("pb", T.pb[:, 0:8 * PS:PS], -BIG)
+    fill("ones", T.ones[:], 1.0)
+    fill("mone7", T.mone7[:], -1.0)
+    fill("nb", T.nb[:], 0.0)
+    fill("ot2", T.ot2[:], 0.0)
+    fill("kf", T.kf[:], 0.0)
+    for nm, m in (("t1", 96), ("t2", 16), ("t3", 31)):
+        vec([R("ip")], [R(nm)], lambda: g.vector.tensor_scalar(T[nm][:, 0:1], T.ip[:, 0:1], m, None, ALU.bitwise_and))
+    for j, nm, s, b in ((0, "t1", 1.0, 16.0), (1, "t1", 1.0, 32.0), (2, "t2", 0.0625, 0.0), (3, "t2", -0.0625, 1.0), (4, "t3", 16.0, 16.0)):
+        vec([R(nm)], [R("col", j, j + 1)], lambda: g.vector.tensor_scalar(T.col[:, j:j + 1], T[nm][:, 0:1], s, b, ALU.mult, ALU.add))
+    vec([R("dd"), R("col", 3, 4)], [R("dde")], lambda: g.vector.tensor_scalar(T.dde[:], T.dd[:], T.col[:, 3:4], None, ALU.mult))
+    vec([R("dd"), R("col", 2, 3)], [R("ddo")], lambda: g.vector.tensor_scalar(T.ddo[:], T.dd[:], T.col[:, 2:3], None, ALU.mult))
+    vec([R("cz")], [R("czt")], lambda: g.vector.transpose(T.czt[:], T.cz[:]))
+    vec([R("czt")], [R("off")], lambda: g.vector.tensor_scalar(T.off[:, 0:6:2], T.czt[:, 0:96:32], 31.0, None, ALU.min))
+    for b in range(4):
+        quant("cf", "scf", 128 * b, 128, "dd", 3 - b, [R("dd")])
+    quant("qx0", "sx0", 0, C, "xin", 0, [R("xin")])
+    quant("qu", "squ", 0, 128, "uin", 0, [R("uin")])
+
+    SB, YB = 6, 7
+    RB = [4, 5, 7, 0]
+    VB = [1, 2, 3, 4]
+    ncol = [16 * (k % 2) + k // 2 for k in range(8)]
+    for r in range(3):
+        last = r == 2
+        X, SX, X1, SX1 = "qx%d" % r, "sx%d" % r, "qx%d" % (r + 1), "sx%d" % (r + 1)
+        U, SU = ("qu", "squ") if r == 0 else ("land%d" % r, "lsc%d" % r)
+        ue, se, uo, so, qz, sz, pk, sk, qv, sv = [n + str(r) for n in ("ue", "se", "uo", "so", "qz", "sz", "pk", "sk", "qv", "sv")]
+
+        def tee(b, j):
+            mm(j, C, "cf", "scf", 128 * b, X, SX, 0, True, False)
+
+        if r:
+            for b in range(4):
+                tee(b, b)
+        for h in range(2):
+            mm(4 + h, 128, X, SX, 96 * h, U, SU, 0, True, True)
+        mm(SB, C, U, SU, 0, X, SX, 0, True, True)
+        if not r:
+            for b in range(4):
+                tee(b, b)
+        tee(2, RB[2])
+        for h in range(2):
+            p0 = 144 * h
+            vec([R("bank%d" % (4 + h)), R("rst")], [R("pa", p0 + 1, p0 + 129)],
+                lambda: g.vector.tensor_tensor_scan(T.pa[:, p0 + 1:p0 + 129], T.rst[:], bank(4 + h, 128), -BIG, ALU.min, ALU.max))
+        for h in range(2):
+            p0 = 144 * h
+            vec([R("bank%d" % (4 + h)), R("pa", p0, p0 + 128)], [R("nr", 128 * h, 128 * h + 128)],
+                lambda: g.vector.tensor_tensor(T.nr[:, 128 * h:128 * h + 128], bank(4 + h, 128), T.pa[:, p0:p0 + 128], ALU.is_le))
+        for b in range(2):
+            tee(b, RB[b])
+        vec([R("nr"), R("mones")], [R("ag")], lambda: g.vector.tensor_tensor_scan(T.ag[:], T.nr[:], T.mones[:], 0.0, ALU.mult, ALU.add))
+        vec([R("ag")], [R("kt")], lambda: g.vector.transpose(T.kt[:], T.ag[:]))
+        dmas("dk", [("s" if h == 0 else "a", [R("kt")], [R("ot", 0, 16)], T.ot[32 * a + 16 * h:32 * a + 16 * h + 16, 0:16],
+                     T.kt[15:128:16, 128 * h + 32 * a:128 * h + 32 * a + 32]) for a in range(4) for h in range(2)])
+        for k in range(8):
+            o = PS * k
+            d1 = [R("bigc")] if k == 0 else [R("pb", o - PS, o - PS + 224)]
+            vec([R("bank%d" % SB)] + d1, [R("pb", o + 1, o + 225)],
+                lambda: g.vector.tensor_tensor_scan(T.pb[:, o + 1:o + 225], bank(SB, C), T.bigc[:] if k == 0 else T.pb[:, o - PS:o - PS + 224], -BIG, ALU.max, ALU.min))
+        vec([R("pb")], [R("eq")], lambda: g.vector.tensor_tensor(T.eq[:, 1:8], T.pb[:, PS + 224:8 * PS:PS], T.pb[:, 224:7 * PS:PS], ALU.is_equal))
+        vec([R("eq"), R("mone7")], [R("ne")], lambda: g.vector.tensor_tensor_scan(T.ne[:, 1:8], T.mone7[:, 0:7], T.eq[:, 1:8], 0.0, ALU.add, ALU.mult))
+        act([R("pb", 0, 225)], [R("nb", ncol[0], ncol[0] + 1), R("junk", 0, C)],
+            lambda: g.scalar.activation(T.junk[:, 0:C], T.pb[:, 1:225], ACT.Sign, bias=T.pb[:, 224:225], scale=-1.0, accum_out=T.nb[:, ncol[0]:ncol[0] + 1]))
+
+        def flags(k):
+            o = PS * k + 224
+            vec([R("bank%d" % SB), R("pb", o, o + 1)], [R("fb", C * k, C * k + C)],
+                lambda: g.vector.tensor_scalar(T.fb[:, C * k:C * k + C], bank(SB, C), T.pb[:, o:o + 1], None, ALU.is_equal))
+
+        def counts(k):
+            vec([R("fb", C * k, C * k + C), R("ne"), R("ones")], [R("cb", C * k, C * k + C)],
+                lambda: g.vector.tensor_tensor_scan(T.cb[:, C * k:C * k + C], T.fb[:, C * k:C * k + C], T.ones[:], T.ne[:, k:k + 1], ALU.add, ALU.min))
+
+        def places(k):
+            act([R("cb", C * k, C * k + C)], [R("nb", ncol[k], ncol[k] + 1), R("junk", C * k, C * k + C)],
+                lambda: g.scalar.activation(T.junk[:, C * k:C * k + C], T.cb[:, C * k:C * k + C], ACT.Sign, bias=1.0, scale=-1.0, accum_out=T.nb[:, ncol[k]:ncol[k] + 1]))
+
+        flags(1)
+        vec([R("ot", 0, 16)], [R("ot", 16, 32)], lambda: g.vector.tensor_copy(T.ot[:, 16:32], T.ot[:, 0:16]))
+        flags(2)
+        vec([R("ot")], [R("ott")], lambda: g.vector.transpose(T.ott[:], T.ot[:]))
+        counts(1)
+        for e in range(2):
+            vec([R("ott"), R("off"), R("col")], [R("lst", 16 * e, 16 * e + 16)],
+                lambda: g.vector.tensor_scalar(T.lst[:, 16 * e:16 * e + 16], T.ott[:, 0:32].indirect(T.off[:, 2 * e:2 * e + 1]), -16.0, T.col[:, e:e + 1], ALU.max, ALU.add))
+        for e, (q, s) in enumerate(((ue, se), (uo, so))):
+            vec([R(U), R("lst", 16 * e, 16 * e + 16)], [R(q)],
+                lambda: g.vector.tensor_copy(T[q][:].bitcast(dt.uint32), T[U][:].bitcast(dt.uint32).indirect(T.lst[:, 16 * e:16 * e + 14])))
+            act([R(SU), R("lst", 16 * e, 16 * e + 16)], [R(s)],
+                lambda: g.scalar.activation(T[s][:], T[SU][:].indirect(T.lst[:, 16 * e:16 * e + 14]), ACT.Copy))
+        if r == 0:
+            for b in range(4):
+                quant("ce", "sce", 128 * b, 128, "dde", 3 - b, [R("dde")])
+            for b in range(4):
+                quant("cd", "scd", 128 * b, 128, "ddo", 3 - b, [R("ddo")])
+        counts(2)
+        for b in range(4):
+            mm(b, C, "ce", "sce", 128 * b, ue, se, 0, False, False)
+        for b in range(4):
+            mm(b, C, "cd", "scd", 128 * b, uo, so, 0, False, True)
+        for b in range(4):
+            act([R("bank%d" % b)], [R("zt%d" % b)], lambda: g.scalar.activation(T.zt[:, b:4 * C:4], bank(b, C), ACT.Copy, scale=2.0 ** -6))
+            places(b + 1)
+            if b + 3 < 8:
+                flags(b + 3)
+                counts(b + 3)
+        for k in (7,):
+            flags(k)
+            counts(k)
+        for k in (5, 6, 7):
+            places(k)
+        tee(3, RB[3])
+        vec([R("nb")], [R("nt")], lambda: g.vector.transpose(T.nt[:], T.nb[:]))
+        dmas("dn", [("s" if a % 2 == 0 else "a", [R("nt")], [R("ot2", 0, 16)], T.ot2[32 * a:32 * a + 16, 0:16], T.nt[a:128:16, 0:32]) for a in range(4)])
+        quant(qz, sz, 0, C, "zt", 0, [R("zt%d" % b) for b in range(4)])
+        if last:
+            for h in range(2):
+                vec([R("ag")], [R("kf", 32 * h, 32 * h + 8)], lambda: g.vector.tensor_copy(T.kf[:, 32 * h:32 * h + 8], T.ag[:, 128 * h + 15:128 * h + 128:16]))
+            vec([R("kf")], [R("kft")], lambda: g.vector.transpose(T.kft[:], T.kf[:]))
+            vec([R("kft"), R("col")], [R("kfo")], lambda: g.vector.tensor_scalar(T.kfo[:], T.kft[:], -16.0, T.col[:, 4:5], ALU.max, ALU.add))
+            jobs = []
+            for A in range(4):
+                for h in range(2):
+                    if h == 0 or A:
+                        jobs.append(("s", [R("kfo")], [], T.op[0:8, 96 * h + 32 * A:96 * h + 32 * A + 32], T.kfo[32 * A:32 * A + 8, 32 * h:32 * h + 32]))
+                for e in range(2):
+                    jobs.append(("s", [R("nt")], [], T.op[e:8:2, 224 + 32 * A:256 + 32 * A], T.nt[32 * A + 16 * e:32 * A + 16 * e + 4, 0:32]))
+            dmas("st", jobs)
+        for b in range(4):
+            mm(RB[b], C, "wq", "wsc", 128 * b, qz, sz, 0, False, True)
+            act([R("bank%d" % RB[b])], [R("xt%d" % b)], lambda: g.scalar.activation(T.xt[:, b:4 * C:4], bank(RB[b], C), ACT.Copy, scale=2.0 ** -5))
+        quant(X1, SX1, 0, C, "xt", 0, [R("xt%d" % b) for b in range(4)])
+        vec([R("ot2", 0, 16)], [R("ot2", 16, 32)], lambda: g.vector.tensor_copy(T.ot2[:, 16:32], T.ot2[:, 0:16]))
+        vec([R("ot2")], [R("ott2")], lambda: g.vector.transpose(T.ott2[:], T.ot2[:]))
+        vec([R("ott2"), R("off")], [R("lst2")], lambda: g.vector.tensor_copy(T.lst2[:], T.ott2[:, 0:32].indirect(T.off[:, 4:5])))
+        vec([R(X1), R("lst2")], [R(pk)], lambda: g.vector.tensor_copy(T[pk][:].bitcast(dt.uint32), T[X1][:].bitcast(dt.uint32).indirect(T.lst2[:, 0:16])))
+        act([R(SX1), R("lst2")], [R(sk)], lambda: g.scalar.activation(T[sk][:], T[SX1][:].indirect(T.lst2[:, 0:16]), ACT.Copy))
+        for b in range(4):
+            mm(VB[b], 128, "ce", "sce", 128 * b, pk, sk, 0, True, False)
+            mm(VB[b], 128, "cd", "scd", 128 * b, pk, sk, 128, False, True)
+            if b % 2 == 0:
+                act([R("bank%d" % VB[b])], [R("vt%d" % b)], lambda: g.scalar.activation(T.vt[:, b:512:4], bank(VB[b], 128), ACT.Copy, scale=2.0 ** -5))
+            else:
+                vec([R("bank%d" % VB[b])], [R("vt%d" % b)], lambda: g.vector.tensor_scalar(T.vt[:, b:512:4], bank(VB[b], 128), 2.0 ** -5, None, ALU.mult))
+        quant(qv, sv, 0, 128, "vt", 0, [R("vt%d" % b) for b in range(4)])
+        dst = T.cores[(rank + STEP[r]) % 8]
+        src = T.cores[(rank - STEP[r]) % 8]
+        rid, pid = topo.addr(dst, core)
+        need("g", deps("g", [R(qv), R(sv)], []))
+        arr = "arr%d" % (r + 1)
+        ld, ls = T["land%d" % (r + 1)], T["lsc%d" % (r + 1)]
+        g.remote_dma(ld[:].bitcast(dt.uint8), T[qv][:].bitcast(dt.uint8), T.sem[arr], T.sem["loc"], pid, rid, topo.mask(core, dst))
+        g.remote_dma(ls[:], T[sv][:], T.sem[arr], T.sem["loc"], pid, rid, topo.mask(core, dst))
+        count["loc"] += 2 * len(topo.engines(core, dst))
+        count[arr] = 2 * len(topo.engines(src, core))
+        tok = (arr, count[arr], {arr: count[arr]})
+        note("g", tok, [], [R("land%d" % (r + 1)), R("lsc%d" % (r + 1))])
+        if r == 0:
+            quant("qvv", "sqvv", 0, 128, "vin", 0, [R("vin")])
+    mm(YB, C, "qvv", "sqvv", 0, "qx3", "sx3", 0, True, True)
+    act([R("bank%d" % YB)], [R("yb")], lambda: g.scalar.activation(T.yb[:], bank(YB, C), ACT.Copy))
+    jobs = [("s", [R("qx3")], [], T.oc[:], T.qx3[:].bitcast(dt.uint8))]
+    jobs += [("s", [R("sx3")], [], T.osc[4 * k:4 * k + 4, :], T.sx3[32 * k:32 * k + 4, :]) for k in range(4)]
+    jobs += [("s", [R("yb")], [], T.y[:], T.yb[:])]
+    dmas("st", jobs)
+    jobs = [("s", [R("land3")], [], T.uc[:], T.land3[:].bitcast(dt.uint8))]
+    jobs += [("a" if k % 2 == 0 else "s", [R("lsc3")], [], T.usc[4 * k:4 * k + 4, :], T.lsc3[32 * k:32 * k + 4, :]) for k in range(4)]
+    dmas("st", jobs)
+    g.wait_ge(T.sem["loc"], count["loc"])
+    for s in ("vs", "ts", "sa", "gc0", "dk", "dn", "ldx", "ldu", "ldv", "ldw", "ldp", "st"):
+        g.sync.wait_ge(T.sem[s], count[s])

@@ -1,6 +1,4 @@
-import numpy as np
-from concourse.bass import DstId, RemoteDMATransfer
-from concourse.mybir import dt, AluOpType, AxisListType, ActivationFunctionType
+from concourse.mybir import dt, AluOpType, ActivationFunctionType
 
 STEP = [4, 1, 2]
 C = 224
@@ -9,6 +7,8 @@ PS = 232
 F8 = "float8_e4m3fn_x4"
 ALU = AluOpType
 ACT = ActivationFunctionType
+SEQ = "s0 s1 p0 s2 s3 n1 n2 n3 f1 s4 f2 n4 s5 f3 s6 D f4 n6 n5 X s7 E q f5 n7 e O c1 p1 Z0 c3 c4 c5 w3 c2 f6 f7 c6 c7 p5 w6 p4 w2 w7 Z2 Z1 P2 P6 Z3 N Q R0 r1 R3 r2"
+NS = [k for k in range(8) if "n%d" % k in SEQ.split()]
 
 SCRATCH = {
     "xin": ("sbuf", [128, 4 * C], "bfloat16"), "uin": ("sbuf", [128, 512], "bfloat16"), "vin": ("sbuf", [128, 512], "bfloat16"),
@@ -22,12 +22,14 @@ SCRATCH = {
     "cd": ("sbuf", [128, 512], F8), "scd": ("sbuf", [128, 512], "uint8"),
     "zt": ("sbuf", [128, 4 * C], "bfloat16"), "xt": ("sbuf", [128, 4 * C], "bfloat16"), "vt": ("sbuf", [128, 512], "bfloat16"),
     "bigc": ("sbuf", [128, C], "float32"), "rst": ("sbuf", [128, 128], "float32"),
-    "mones": ("sbuf", [128, 256], "bfloat16"), "ones": ("sbuf", [128, C], "bfloat16"), "mone7": ("sbuf", [128, 8], "float32"),
+    "mones": ("sbuf", [128, 256], "bfloat16"), "ones": ("sbuf", [128, C], "bfloat16"), "zeros": ("sbuf", [128, C], "bfloat16"),
+    "mone7": ("sbuf", [128, 8], "float32"),
     "pa": ("sbuf", [128, 288], "float32"), "nr": ("sbuf", [128, 256], "bfloat16"), "ag": ("sbuf", [128, 256], "bfloat16"),
     "kt": ("sbuf", [128, 256], "bfloat16"), "ot": ("sbuf", [128, 32], "bfloat16"), "ott": ("sbuf", [128, 32], "bfloat16"),
     "lst": ("sbuf", [128, 32], "uint16"),
     "pb": ("sbuf", [128, 8 * PS], "float32"), "eq": ("sbuf", [128, 8], "float32"), "ne": ("sbuf", [128, 8], "float32"),
-    "fb": ("sbuf", [128, 8 * C], "bfloat16"), "cb": ("sbuf", [128, 8 * C], "bfloat16"), "junk": ("sbuf", [128, 8 * C], "bfloat16"),
+    "sg": ("sbuf", [128, 8 * C], "bfloat16"), "fb": ("sbuf", [128, 8 * C], "bfloat16"),
+    "cb": ("sbuf", [128, 8 * C], "bfloat16"), "junk": ("sbuf", [128, 8 * C], "bfloat16"),
     "nb": ("sbuf", [128, 32], "float32"), "nt": ("sbuf", [128, 32], "float32"),
     "ot2": ("sbuf", [128, 32], "float32"), "ott2": ("sbuf", [128, 32], "float32"), "lst2": ("sbuf", [128, 16], "uint16"),
     "ip": ("sbuf", [128, 2], "int32"), "t1": ("sbuf", [128, 2], "int32"), "t2": ("sbuf", [128, 2], "int32"), "t3": ("sbuf", [128, 2], "int32"),
@@ -41,12 +43,9 @@ for _r in range(4):
     SCRATCH["qx%d" % _r] = ("sbuf", [128, C], F8)
     SCRATCH["sx%d" % _r] = ("sbuf", [128, C], "uint8")
 for _r in range(3):
-    SCRATCH["ue%d" % _r] = ("sbuf", [128, C], F8)
-    SCRATCH["se%d" % _r] = ("sbuf", [128, C], "uint8")
-    SCRATCH["uo%d" % _r] = ("sbuf", [128, C], F8)
-    SCRATCH["so%d" % _r] = ("sbuf", [128, C], "uint8")
-    SCRATCH["qz%d" % _r] = ("sbuf", [128, C], F8)
-    SCRATCH["sz%d" % _r] = ("sbuf", [128, C], "uint8")
+    for _q, _s in (("ue", "se"), ("uo", "so"), ("qz", "sz")):
+        SCRATCH["%s%d" % (_q, _r)] = ("sbuf", [128, C], F8)
+        SCRATCH["%s%d" % (_s, _r)] = ("sbuf", [128, C], "uint8")
     SCRATCH["pk%d" % _r] = ("sbuf", [128, 256], F8)
     SCRATCH["sk%d" % _r] = ("sbuf", [128, 256], "uint8")
     SCRATCH["qv%d" % _r] = ("sbuf", [128, 128], F8)
@@ -153,14 +152,20 @@ def rank_program(g, core, T, topo):
     def fill(name, view, c, lo=0, hi=None):
         vec([], [R(name, lo, hi)], lambda: g.vector.memset(view, c))
 
+    def iota(name, view, pat, base, lo=0, hi=None):
+        run("g", [], [R(name, lo, hi)], lambda: g.iota(view, pat, base, 0, allow_small_or_imprecise_dtypes=True))
+
     def quant(q, s, lo, n, tile, tlo, names):
         vec(names, [R(q, lo, lo + n), R(s, lo, lo + n)], lambda: g.vector.quantize_mx(T[q][:, lo:lo + n], T[s][:, lo:lo + n], T[tile][:, tlo:tlo + 4 * n]))
 
-    dmas("ldx", [("s", [], [R("xin")], T.xin[:], T.x[:])])
+    def column(j, nm, sc, b):
+        vec([R(nm)], [R("col", j, j + 1)], lambda: g.vector.tensor_scalar(T.col[:, j:j + 1], T[nm][:, 0:1], sc, b, ALU.mult, ALU.add))
+
+    def bits(nm, m):
+        vec([R("ip")], [R(nm)], lambda: g.vector.tensor_scalar(T[nm][:, 0:1], T.ip[:, 0:1], m, None, ALU.bitwise_and))
+
+    xtok = dmas("ldx", [("s", [], [R("xin")], T.xin[:], T.x[:])])
     dmas("ldu", [("a", [], [R("uin")], T.uin[:], T.u[:])])
-    dmas("ldw", [("s", [], [R("wq")], T.wq[:].bitcast(dt.uint8), T.wc[:])])
-    dmas("ldp", [("a", [], [R("wsc")], T.wsc[:], T.ws[:])])
-    dmas("ldv", [("s", [], [R("vin")], T.vin[:], T.v[:])])
 
     fill("c32", T.c32[:], 32.0)
     run("g", [], [R("ip")], lambda: g.iota(T.ip[:, 0:1], [[0, 1]], 0, 1))
@@ -168,34 +173,45 @@ def rank_program(g, core, T, topo):
     for blk, base, pat in ((0, 0, [[20, 2], [4, 4], [1, 2]]), (1, 2, [[20, 2], [4, 4], [1, 2]]), (2, 0, [[2, 2], [4, 4], [1, 2]])):
         for h in range(2):
             lo = 32 * blk + 16 * h
-            run("g", [], [R("cz", lo, lo + 16)], lambda: g.iota(T.cz[:, lo:lo + 16], pat, base, 0, allow_small_or_imprecise_dtypes=True))
+            iota("cz", T.cz[:, lo:lo + 16], pat, base, lo, lo + 16)
+    iota("mones", T.mones[:], [[0, 256]], -1)
+    iota("mone7", T.mone7[:], [[0, 8]], -1)
+    iota("ones", T.ones[:], [[0, C]], 1)
+    iota("zeros", T.zeros[:], [[0, C]], 0)
+    iota("nb", T.nb[:], [[0, 32]], 0)
+    iota("ot2", T.ot2[:], [[0, 32]], 0)
+    iota("kf", T.kf[:], [[0, 64]], 0)
     fill("rst", T.rst[:], BIG)
+    bits("t2", 16)
+    bits("t1", 96)
+    bits("t3", 31)
+    column(3, "t2", -0.0625, 1.0)
+    column(2, "t2", 0.0625, 0.0)
+    column(0, "t1", 1.0, 16.0)
+    column(1, "t1", 1.0, 32.0)
+    column(4, "t3", 16.0, 16.0)
+    act([R("dd"), R("col", 3, 4)], [R("dde")], lambda: g.scalar.activation(T.dde[:], T.dd[:], ACT.Copy, scale=T.col[:, 3:4]))
+    act([R("dd"), R("col", 2, 3)], [R("ddo")], lambda: g.scalar.activation(T.ddo[:], T.dd[:], ACT.Copy, scale=T.col[:, 2:3]))
     fill("rst", T.rst[:, 0:128:16], -BIG)
     fill("pa", T.pa[:, 0:288:144], -BIG, 0, 1)
-    fill("mones", T.mones[:], -1.0)
-    fill("bigc", T.bigc[:], BIG)
     fill("pb", T.pb[:, 0:8 * PS:PS], -BIG)
-    fill("ones", T.ones[:], 1.0)
-    fill("mone7", T.mone7[:], -1.0)
-    fill("nb", T.nb[:], 0.0)
-    fill("ot2", T.ot2[:], 0.0)
-    fill("kf", T.kf[:], 0.0)
-    for nm, m in (("t1", 96), ("t2", 16), ("t3", 31)):
-        vec([R("ip")], [R(nm)], lambda: g.vector.tensor_scalar(T[nm][:, 0:1], T.ip[:, 0:1], m, None, ALU.bitwise_and))
-    for j, nm, s, b in ((0, "t1", 1.0, 16.0), (1, "t1", 1.0, 32.0), (2, "t2", 0.0625, 0.0), (3, "t2", -0.0625, 1.0), (4, "t3", 16.0, 16.0)):
-        vec([R(nm)], [R("col", j, j + 1)], lambda: g.vector.tensor_scalar(T.col[:, j:j + 1], T[nm][:, 0:1], s, b, ALU.mult, ALU.add))
-    vec([R("dd"), R("col", 3, 4)], [R("dde")], lambda: g.vector.tensor_scalar(T.dde[:], T.dd[:], T.col[:, 3:4], None, ALU.mult))
-    vec([R("dd"), R("col", 2, 3)], [R("ddo")], lambda: g.vector.tensor_scalar(T.ddo[:], T.dd[:], T.col[:, 2:3], None, ALU.mult))
-    vec([R("cz")], [R("czt")], lambda: g.vector.transpose(T.czt[:], T.cz[:]))
-    vec([R("czt")], [R("off")], lambda: g.vector.tensor_scalar(T.off[:, 0:6:2], T.czt[:, 0:96:32], 31.0, None, ALU.min))
+    fill("bigc", T.bigc[:], BIG)
     for b in range(4):
         quant("cf", "scf", 128 * b, 128, "dd", 3 - b, [R("dd")])
-    quant("qx0", "sx0", 0, C, "xin", 0, [R("xin")])
+    for b in range(4):
+        quant("ce", "sce", 128 * b, 128, "dde", 3 - b, [R("dde")])
     quant("qu", "squ", 0, 128, "uin", 0, [R("uin")])
+    for b in range(4):
+        quant("cd", "scd", 128 * b, 128, "ddo", 3 - b, [R("ddo")])
+    quant("qx0", "sx0", 0, C, "xin", 0, [R("xin")])
+    need("s", [xtok])
+    dmas("ldw", [("s", [], [R("wq")], T.wq[:].bitcast(dt.uint8), T.wc[:])])
+    dmas("ldp", [("s", [], [R("wsc")], T.wsc[:], T.ws[:])])
+    dmas("ldv", [("s", [], [R("vin")], T.vin[:], T.v[:])])
 
-    SB, YB = 6, 7
-    RB = [4, 5, 7, 0]
-    VB = [1, 2, 3, 4]
+    SB, SB2, YB = 6, 7, 7
+    RB = [4, 5, 0, 1]
+    VB = [2, 3, 4, 5]
     ncol = [16 * (k % 2) + k // 2 for k in range(8)]
     for r in range(3):
         last = r == 2
@@ -212,10 +228,10 @@ def rank_program(g, core, T, topo):
         for h in range(2):
             mm(4 + h, 128, X, SX, 96 * h, U, SU, 0, True, True)
         mm(SB, C, U, SU, 0, X, SX, 0, True, True)
+        mm(SB2, C, U, SU, 0, X, SX, 0, True, True)
         if not r:
             for b in range(4):
                 tee(b, b)
-        tee(2, RB[2])
         for h in range(2):
             p0 = 144 * h
             vec([R("bank%d" % (4 + h)), R("rst")], [R("pa", p0 + 1, p0 + 129)],
@@ -227,95 +243,118 @@ def rank_program(g, core, T, topo):
         for b in range(2):
             tee(b, RB[b])
         vec([R("nr"), R("mones")], [R("ag")], lambda: g.vector.tensor_tensor_scan(T.ag[:], T.nr[:], T.mones[:], 0.0, ALU.mult, ALU.add))
+        if not r:
+            vec([R("cz")], [R("czt")], lambda: g.vector.transpose(T.czt[:], T.cz[:]))
         vec([R("ag")], [R("kt")], lambda: g.vector.transpose(T.kt[:], T.ag[:]))
         dmas("dk", [("s" if h == 0 else "a", [R("kt")], [R("ot", 0, 16)], T.ot[32 * a + 16 * h:32 * a + 16 * h + 16, 0:16],
                      T.kt[15:128:16, 128 * h + 32 * a:128 * h + 32 * a + 32]) for a in range(4) for h in range(2)])
-        for k in range(8):
+        if not r:
+            vec([R("czt")], [R("off")], lambda: g.vector.tensor_scalar(T.off[:, 0:6:2], T.czt[:, 0:96:32], 31.0, None, ALU.min))
+
+        def scan(k):
             o = PS * k
             d1 = [R("bigc")] if k == 0 else [R("pb", o - PS, o - PS + 224)]
             vec([R("bank%d" % SB)] + d1, [R("pb", o + 1, o + 225)],
                 lambda: g.vector.tensor_tensor_scan(T.pb[:, o + 1:o + 225], bank(SB, C), T.bigc[:] if k == 0 else T.pb[:, o - PS:o - PS + 224], -BIG, ALU.max, ALU.min))
-        vec([R("pb")], [R("eq")], lambda: g.vector.tensor_tensor(T.eq[:, 1:8], T.pb[:, PS + 224:8 * PS:PS], T.pb[:, 224:7 * PS:PS], ALU.is_equal))
-        vec([R("eq"), R("mone7")], [R("ne")], lambda: g.vector.tensor_tensor_scan(T.ne[:, 1:8], T.mone7[:, 0:7], T.eq[:, 1:8], 0.0, ALU.add, ALU.mult))
-        act([R("pb", 0, 225)], [R("nb", ncol[0], ncol[0] + 1), R("junk", 0, C)],
-            lambda: g.scalar.activation(T.junk[:, 0:C], T.pb[:, 1:225], ACT.Sign, bias=T.pb[:, 224:225], scale=-1.0, accum_out=T.nb[:, ncol[0]:ncol[0] + 1]))
+
+        def sign(k):
+            o = PS * k + 224
+            act([R("bank%d" % SB2), R("pb", o, o + 1)], [R("sg", C * k, C * k + C)],
+                lambda: g.scalar.activation(T.sg[:, C * k:C * k + C], bank(SB2, C), ACT.Sign, bias=T.pb[:, o:o + 1], scale=-1.0))
 
         def flags(k):
             o = PS * k + 224
-            vec([R("bank%d" % SB), R("pb", o, o + 1)], [R("fb", C * k, C * k + C)],
-                lambda: g.vector.tensor_scalar(T.fb[:, C * k:C * k + C], bank(SB, C), T.pb[:, o:o + 1], None, ALU.is_equal))
+            if k in NS:
+                vec([R("sg", C * k, C * k + C)], [R("fb", C * k, C * k + C)],
+                    lambda: g.vector.tensor_scalar(T.fb[:, C * k:C * k + C], T.sg[:, C * k:C * k + C], 0.0, None, ALU.is_equal))
+            else:
+                vec([R("bank%d" % SB), R("pb", o, o + 1)], [R("fb", C * k, C * k + C)],
+                    lambda: g.vector.tensor_scalar(T.fb[:, C * k:C * k + C], bank(SB, C), T.pb[:, o:o + 1], None, ALU.is_equal))
+
+        def same(k):
+            vec([R("pb")], [R("eq")], lambda: g.vector.tensor_tensor(T.eq[:, 1:8], T.pb[:, PS + 224:8 * PS:PS], T.pb[:, 224:7 * PS:PS], ALU.is_equal))
+
+        def less(k):
+            vec([R("eq"), R("mone7")], [R("ne")], lambda: g.vector.tensor_tensor_scan(T.ne[:, 1:8], T.mone7[:, 0:7], T.eq[:, 1:8], 0.0, ALU.add, ALU.mult))
 
         def counts(k):
             vec([R("fb", C * k, C * k + C), R("ne"), R("ones")], [R("cb", C * k, C * k + C)],
                 lambda: g.vector.tensor_tensor_scan(T.cb[:, C * k:C * k + C], T.fb[:, C * k:C * k + C], T.ones[:], T.ne[:, k:k + 1], ALU.add, ALU.min))
 
         def places(k):
-            act([R("cb", C * k, C * k + C)], [R("nb", ncol[k], ncol[k] + 1), R("junk", C * k, C * k + C)],
-                lambda: g.scalar.activation(T.junk[:, C * k:C * k + C], T.cb[:, C * k:C * k + C], ACT.Sign, bias=1.0, scale=-1.0, accum_out=T.nb[:, ncol[k]:ncol[k] + 1]))
+            if k == 0:
+                act([R("pb", 0, 225)], [R("nb", ncol[0], ncol[0] + 1), R("junk", 0, C)],
+                    lambda: g.scalar.activation(T.junk[:, 0:C], T.pb[:, 1:225], ACT.Sign, bias=T.pb[:, 224:225], scale=-1.0, accum_out=T.nb[:, ncol[0]:ncol[0] + 1]))
+            else:
+                act([R("cb", C * k, C * k + C)], [R("nb", ncol[k], ncol[k] + 1), R("junk", C * k, C * k + C)],
+                    lambda: g.scalar.activation(T.junk[:, C * k:C * k + C], T.cb[:, C * k:C * k + C], ACT.Sign, bias=1.0, scale=-1.0, accum_out=T.nb[:, ncol[k]:ncol[k] + 1]))
 
-        flags(1)
-        vec([R("ot", 0, 16)], [R("ot", 16, 32)], lambda: g.vector.tensor_copy(T.ot[:, 16:32], T.ot[:, 0:16]))
-        flags(2)
-        vec([R("ot")], [R("ott")], lambda: g.vector.transpose(T.ott[:], T.ot[:]))
-        counts(1)
-        for e in range(2):
+        def rest(k):
+            vec([R("cb", C * k, C * k + C), R("zeros")], [R("junk", C * k, C * k + C)],
+                lambda: g.vector.tensor_tensor_scan(T.junk[:, C * k:C * k + C], T.cb[:, C * k:C * k + C], T.zeros[:], 0.0, ALU.add, ALU.max))
+
+        def pair(k):
+            vec([R("junk", C * k, C * k + 2 * C)], [R("nb", ncol[k], ncol[k] + 1), R("nb", ncol[k + 1], ncol[k + 1] + 1)],
+                lambda: g.vector.tensor_scalar(T.nb[:, ncol[k]:ncol[k + 1] + 1:16], T.junk[:, C * k + C - 1:C * k + 2 * C:C], -1.0, float(C), ALU.mult, ALU.add))
+
+        def halves(k):
+            vec([R("ot", 0, 16)], [R("ot", 16, 32)], lambda: g.vector.tensor_copy(T.ot[:, 16:32], T.ot[:, 0:16]))
+
+        def turn(k):
+            vec([R("ot")], [R("ott")], lambda: g.vector.transpose(T.ott[:], T.ot[:]))
+
+        def picks(e):
+            q, s = ((ue, se), (uo, so))[e]
             vec([R("ott"), R("off"), R("col")], [R("lst", 16 * e, 16 * e + 16)],
                 lambda: g.vector.tensor_scalar(T.lst[:, 16 * e:16 * e + 16], T.ott[:, 0:32].indirect(T.off[:, 2 * e:2 * e + 1]), -16.0, T.col[:, e:e + 1], ALU.max, ALU.add))
-        for e, (q, s) in enumerate(((ue, se), (uo, so))):
             vec([R(U), R("lst", 16 * e, 16 * e + 16)], [R(q)],
                 lambda: g.vector.tensor_copy(T[q][:].bitcast(dt.uint32), T[U][:].bitcast(dt.uint32).indirect(T.lst[:, 16 * e:16 * e + 14])))
             act([R(SU), R("lst", 16 * e, 16 * e + 16)], [R(s)],
                 lambda: g.scalar.activation(T[s][:], T[SU][:].indirect(T.lst[:, 16 * e:16 * e + 14]), ACT.Copy))
-        if r == 0:
             for b in range(4):
-                quant("ce", "sce", 128 * b, 128, "dde", 3 - b, [R("dde")])
-            for b in range(4):
-                quant("cd", "scd", 128 * b, 128, "ddo", 3 - b, [R("ddo")])
-        counts(2)
-        for b in range(4):
-            mm(b, C, "ce", "sce", 128 * b, ue, se, 0, False, False)
-        for b in range(4):
-            mm(b, C, "cd", "scd", 128 * b, uo, so, 0, False, True)
-        for b in range(4):
+                mm(b, C, ("ce", "cd")[e], ("sce", "scd")[e], 128 * b, q, s, 0, False, e == 1)
+
+        def zed(b):
             act([R("bank%d" % b)], [R("zt%d" % b)], lambda: g.scalar.activation(T.zt[:, b:4 * C:4], bank(b, C), ACT.Copy, scale=2.0 ** -6))
-            places(b + 1)
-            if b + 3 < 8:
-                flags(b + 3)
-                counts(b + 3)
-        for k in (7,):
-            flags(k)
-            counts(k)
-        for k in (5, 6, 7):
-            places(k)
-        tee(3, RB[3])
-        vec([R("nb")], [R("nt")], lambda: g.vector.transpose(T.nt[:], T.nb[:]))
-        dmas("dn", [("s" if a % 2 == 0 else "a", [R("nt")], [R("ot2", 0, 16)], T.ot2[32 * a:32 * a + 16, 0:16], T.nt[a:128:16, 0:32]) for a in range(4)])
-        quant(qz, sz, 0, C, "zt", 0, [R("zt%d" % b) for b in range(4)])
-        if last:
-            for h in range(2):
-                vec([R("ag")], [R("kf", 32 * h, 32 * h + 8)], lambda: g.vector.tensor_copy(T.kf[:, 32 * h:32 * h + 8], T.ag[:, 128 * h + 15:128 * h + 128:16]))
-            vec([R("kf")], [R("kft")], lambda: g.vector.transpose(T.kft[:], T.kf[:]))
-            vec([R("kft"), R("col")], [R("kfo")], lambda: g.vector.tensor_scalar(T.kfo[:], T.kft[:], -16.0, T.col[:, 4:5], ALU.max, ALU.add))
-            jobs = []
-            for A in range(4):
-                for h in range(2):
-                    if h == 0 or A:
-                        jobs.append(("s", [R("kfo")], [], T.op[0:8, 96 * h + 32 * A:96 * h + 32 * A + 32], T.kfo[32 * A:32 * A + 8, 32 * h:32 * h + 32]))
-                for e in range(2):
-                    jobs.append(("s", [R("nt")], [], T.op[e:8:2, 224 + 32 * A:256 + 32 * A], T.nt[32 * A + 16 * e:32 * A + 16 * e + 4, 0:32]))
-            dmas("st", jobs)
-        for b in range(4):
-            mm(RB[b], C, "wq", "wsc", 128 * b, qz, sz, 0, False, True)
+
+        def zedv(b):
+            vec([R("bank%d" % b)], [R("zt%d" % b)], lambda: g.vector.tensor_scalar(T.zt[:, b:4 * C:4], bank(b, C), 2.0 ** -6, None, ALU.mult))
+
+        def send_lists(k):
+            vec([R("nb")], [R("nt")], lambda: g.vector.transpose(T.nt[:], T.nb[:]))
+            dmas("dn", [("sa"[h], [R("nt")], [R("ot2", 16 * h, 16 * h + 16)], T.ot2[32 * a:32 * a + 16, 16 * h:16 * h + 16], T.nt[a:128:16, 0:32])
+                        for a in range(4) for h in range(2)])
+
+        def state(k):
+            for b in (2, 3):
+                tee(b, RB[b])
+            quant(qz, sz, 0, C, "zt", 0, [R("zt%d" % b) for b in range(4)])
+            for b in range(4):
+                mm(RB[b], C, "wq", "wsc", 128 * b, qz, sz, 0, False, True)
+
+        def newx(b):
             act([R("bank%d" % RB[b])], [R("xt%d" % b)], lambda: g.scalar.activation(T.xt[:, b:4 * C:4], bank(RB[b], C), ACT.Copy, scale=2.0 ** -5))
+
+        def newxv(b):
+            vec([R("bank%d" % RB[b])], [R("xt%d" % b)], lambda: g.vector.tensor_scalar(T.xt[:, b:4 * C:4], bank(RB[b], C), 2.0 ** -5, None, ALU.mult))
+
+        steps = {"s": scan, "n": sign, "f": flags, "q": same, "e": less, "c": counts, "p": places, "w": rest, "P": pair,
+                 "D": halves, "X": turn, "E": lambda k: picks(0), "O": lambda k: picks(1), "Z": zed, "z": zedv,
+                 "N": send_lists, "Q": state, "R": newx, "r": newxv}
+        for word in SEQ.split():
+            steps[word[0]](int(word[1:] or "0"))
         quant(X1, SX1, 0, C, "xt", 0, [R("xt%d" % b) for b in range(4)])
-        vec([R("ot2", 0, 16)], [R("ot2", 16, 32)], lambda: g.vector.tensor_copy(T.ot2[:, 16:32], T.ot2[:, 0:16]))
         vec([R("ot2")], [R("ott2")], lambda: g.vector.transpose(T.ott2[:], T.ot2[:]))
         vec([R("ott2"), R("off")], [R("lst2")], lambda: g.vector.tensor_copy(T.lst2[:], T.ott2[:, 0:32].indirect(T.off[:, 4:5])))
-        vec([R(X1), R("lst2")], [R(pk)], lambda: g.vector.tensor_copy(T[pk][:].bitcast(dt.uint32), T[X1][:].bitcast(dt.uint32).indirect(T.lst2[:, 0:16])))
-        act([R(SX1), R("lst2")], [R(sk)], lambda: g.scalar.activation(T[sk][:], T[SX1][:].indirect(T.lst2[:, 0:16]), ACT.Copy))
+        for e in range(2):
+            lo = 128 * e
+            vec([R(X1), R("lst2")], [R(pk, lo, lo + 128)],
+                lambda: g.vector.tensor_copy(T[pk][:, lo:lo + 128].bitcast(dt.uint32), T[X1][:].bitcast(dt.uint32).indirect(T.lst2[:, 8 * e:8 * e + 8])))
+            act([R(SX1), R("lst2")], [R(sk, lo, lo + 128)],
+                lambda: g.scalar.activation(T[sk][:, lo:lo + 128], T[SX1][:].indirect(T.lst2[:, 8 * e:8 * e + 8]), ACT.Copy))
+            for b in range(4):
+                mm(VB[b], 128, ("ce", "cd")[e], ("sce", "scd")[e], 128 * b, pk, sk, lo, e == 0, e == 1)
         for b in range(4):
-            mm(VB[b], 128, "ce", "sce", 128 * b, pk, sk, 0, True, False)
-            mm(VB[b], 128, "cd", "scd", 128 * b, pk, sk, 128, False, True)
             if b % 2 == 0:
                 act([R("bank%d" % VB[b])], [R("vt%d" % b)], lambda: g.scalar.activation(T.vt[:, b:512:4], bank(VB[b], 128), ACT.Copy, scale=2.0 ** -5))
             else:
@@ -331,18 +370,28 @@ def rank_program(g, core, T, topo):
         g.remote_dma(ls[:], T[sv][:], T.sem[arr], T.sem["loc"], pid, rid, topo.mask(core, dst))
         count["loc"] += 2 * len(topo.engines(core, dst))
         count[arr] = 2 * len(topo.engines(src, core))
-        tok = (arr, count[arr], {arr: count[arr]})
-        note("g", tok, [], [R("land%d" % (r + 1)), R("lsc%d" % (r + 1))])
+        note("g", (arr, count[arr], {arr: count[arr]}), [], [R("land%d" % (r + 1)), R("lsc%d" % (r + 1))])
         if r == 0:
             quant("qvv", "sqvv", 0, 128, "vin", 0, [R("vin")])
+    for h in range(2):
+        vec([R("ag")], [R("kf", 32 * h, 32 * h + 8)], lambda: g.vector.tensor_copy(T.kf[:, 32 * h:32 * h + 8], T.ag[:, 128 * h + 15:128 * h + 128:16]))
+    vec([R("kf")], [R("kft")], lambda: g.vector.transpose(T.kft[:], T.kf[:]))
+    vec([R("kft"), R("col")], [R("kfo")], lambda: g.vector.tensor_scalar(T.kfo[:], T.kft[:], -16.0, T.col[:, 4:5], ALU.max, ALU.add))
     mm(YB, C, "qvv", "sqvv", 0, "qx3", "sx3", 0, True, True)
     act([R("bank%d" % YB)], [R("yb")], lambda: g.scalar.activation(T.yb[:], bank(YB, C), ACT.Copy))
     jobs = [("s", [R("qx3")], [], T.oc[:], T.qx3[:].bitcast(dt.uint8))]
     jobs += [("s", [R("sx3")], [], T.osc[4 * k:4 * k + 4, :], T.sx3[32 * k:32 * k + 4, :]) for k in range(4)]
-    jobs += [("s", [R("yb")], [], T.y[:], T.yb[:])]
+    for A in range(4):
+        for e in range(2):
+            jobs.append(("s", [R("nt")], [], T.op[e:8:2, 224 + 32 * A:256 + 32 * A], T.nt[32 * A + 16 * e:32 * A + 16 * e + 4, 0:32]))
+    jobs.append(("s", [R("yb")], [], T.y[:], T.yb[:]))
+    for A in range(4):
+        for h in range(2):
+            if h == 0 or A:
+                jobs.append(("s", [R("kfo")], [], T.op[0:8, 96 * h + 32 * A:96 * h + 32 * A + 32], T.kfo[32 * A:32 * A + 8, 32 * h:32 * h + 32]))
     dmas("st", jobs)
     jobs = [("s", [R("land3")], [], T.uc[:], T.land3[:].bitcast(dt.uint8))]
-    jobs += [("a" if k % 2 == 0 else "s", [R("lsc3")], [], T.usc[4 * k:4 * k + 4, :], T.lsc3[32 * k:32 * k + 4, :]) for k in range(4)]
+    jobs += [("as"[k % 2], [R("lsc3")], [], T.usc[4 * k:4 * k + 4, :], T.lsc3[32 * k:32 * k + 4, :]) for k in range(4)]
     dmas("st", jobs)
     g.wait_ge(T.sem["loc"], count["loc"])
     for s in ("vs", "ts", "sa", "gc0", "dk", "dn", "ldx", "ldu", "ldv", "ldw", "ldp", "st"):

from concourse.mybir import dt, AluOpType, ActivationFunctionType

STEP = [4, 1, 2]
C = 224
BIG = 1.0e29
PS = 232
F8 = "float8_e4m3fn_x4"
ALU = AluOpType
ACT = ActivationFunctionType
SEQ = "s0 s1 p0 s2 s3 n1 n2 n3 f1 s4 f2 n4 s5 f3 s6 D f4 n6 n5 X s7 E q f5 n7 e O c1 p1 Z0 c3 c4 c5 w3 c2 f6 f7 c6 c7 p5 w6 p4 w2 w7 Z2 Z1 P2 P6 Z3 N Q R0 r1 R3 r2"
NS = [k for k in range(8) if "n%d" % k in SEQ.split()]

SCRATCH = {
    "xin": ("sbuf", [128, 4 * C], "bfloat16"), "uin": ("sbuf", [128, 512], "bfloat16"), "vin": ("sbuf", [128, 512], "bfloat16"),
    "wq": ("sbuf", [128, 512], F8), "wsc": ("sbuf", [128, 512], "uint8"),
    "qu": ("sbuf", [128, 128], F8), "squ": ("sbuf", [128, 128], "uint8"),
    "qvv": ("sbuf", [128, 128], F8), "sqvv": ("sbuf", [128, 128], "uint8"),
    "c32": ("sbuf", [128, 516], "bfloat16"), "dd": ("sbuf", [128, 516], "bfloat16"),
    "dde": ("sbuf", [128, 516], "bfloat16"), "ddo": ("sbuf", [128, 516], "bfloat16"),
    "cf": ("sbuf", [128, 512], F8), "scf": ("sbuf", [128, 512], "uint8"),
    "ce": ("sbuf", [128, 512], F8), "sce": ("sbuf", [128, 512], "uint8"),
    "cd": ("sbuf", [128, 512], F8), "scd": ("sbuf", [128, 512], "uint8"),
    "zt": ("sbuf", [128, 4 * C], "bfloat16"), "xt": ("sbuf", [128, 4 * C], "bfloat16"), "vt": ("sbuf", [128, 512], "bfloat16"),
    "bigc": ("sbuf", [128, C], "float32"), "rst": ("sbuf", [128, 128], "float32"),
    "mones": ("sbuf", [128, 256], "bfloat16"), "ones": ("sbuf", [128, C], "bfloat16"), "zeros": ("sbuf", [128, C], "bfloat16"),
    "mone7": ("sbuf", [128, 8], "float32"),
    "pa": ("sbuf", [128, 288], "float32"), "nr": ("sbuf", [128, 256], "bfloat16"), "ag": ("sbuf", [128, 256], "bfloat16"),
    "kt": ("sbuf", [128, 256], "bfloat16"), "ot": ("sbuf", [128, 32], "bfloat16"), "ott": ("sbuf", [128, 32], "bfloat16"),
    "lst": ("sbuf", [128, 32], "uint16"),
    "pb": ("sbuf", [128, 8 * PS], "float32"), "eq": ("sbuf", [128, 8], "float32"), "ne": ("sbuf", [128, 8], "float32"),
    "sg": ("sbuf", [128, 8 * C], "bfloat16"), "fb": ("sbuf", [128, 8 * C], "bfloat16"),
    "cb": ("sbuf", [128, 8 * C], "bfloat16"), "junk": ("sbuf", [128, 8 * C], "bfloat16"),
    "nb": ("sbuf", [128, 32], "float32"), "nt": ("sbuf", [128, 32], "float32"),
    "ot2": ("sbuf", [128, 32], "float32"), "ott2": ("sbuf", [128, 32], "float32"), "lst2": ("sbuf", [128, 16], "uint16"),
    "ip": ("sbuf", [128, 2], "int32"), "t1": ("sbuf", [128, 2], "int32"), "t2": ("sbuf", [128, 2], "int32"), "t3": ("sbuf", [128, 2], "int32"),
    "col": ("sbuf", [128, 8], "float32"),
    "cz": ("sbuf", [128, 96], "float32"), "czt": ("sbuf", [128, 96], "float32"), "off": ("sbuf", [128, 8], "uint16"),
    "kf": ("sbuf", [128, 64], "float32"), "kft": ("sbuf", [128, 64], "float32"), "kfo": ("sbuf", [128, 64], "float32"),
    "yb": ("sbuf", [128, C], "float32"),
    "ps": ("psum", [128, 4096], "float32"),
}
for _r in range(4):
    SCRATCH["qx%d" % _r] = ("sbuf", [128, C], F8)
    SCRATCH["sx%d" % _r] = ("sbuf", [128, C], "uint8")
for _r in range(3):
    for _q, _s in (("ue", "se"), ("uo", "so"), ("qz", "sz")):
        SCRATCH["%s%d" % (_q, _r)] = ("sbuf", [128, C], F8)
        SCRATCH["%s%d" % (_s, _r)] = ("sbuf", [128, C], "uint8")
    SCRATCH["pk%d" % _r] = ("sbuf", [128, 256], F8)
    SCRATCH["sk%d" % _r] = ("sbuf", [128, 256], "uint8")
    SCRATCH["qv%d" % _r] = ("sbuf", [128, 128], F8)
    SCRATCH["sv%d" % _r] = ("sbuf", [128, 128], "uint8")
    SCRATCH["land%d" % (_r + 1)] = ("sbuf", [128, 128], F8)
    SCRATCH["lsc%d" % (_r + 1)] = ("sbuf", [128, 128], "uint8")
SEMAPHORES = ["vs", "ts", "sa", "gc0", "dk", "dn", "ldx", "ldu", "ldv", "ldw", "ldp", "loc", "arr1", "arr2", "arr3", "st"]


def rank_program(g, core, T, topo):
    rank = T.rank_of(core)
    if rank is None:
        return
    queue = {"v": g.vector, "t": g.tensor, "a": g.scalar, "s": g.sync, "g": g}
    csem = {"v": "vs", "t": "ts", "a": "sa", "g": "gc0"}
    known = {q: {} for q in queue}
    count = {s: 0 for s in SEMAPHORES}
    clocks = {s: {} for s in SEMAPHORES}
    regs = {}

    def merge(a, b):
        for s, n in b.items():
            if a.get(s, 0) < n:
                a[s] = n

    def deps(q, reads, writes):
        out = []
        for w, items in ((False, reads), (True, writes)):
            for name, lo, hi in items:
                bank = name.startswith("bank")
                for (l, h, ww, qq, tok) in regs.get(name, []):
                    if l >= hi or h <= lo:
                        continue
                    if bank:
                        if qq == q and (q == "t" or not (w or ww)):
                            continue
                    elif not (w or ww):
                        continue
                    out.append(tok)
        return out

    def need(q, toks):
        best = {}
        for tk in toks:
            s, n, c = tk
            if known[q].get(s, 0) < n and (s not in best or best[s][1] < n):
                best[s] = tk
        for s in list(best):
            if any(o != s and best[o][2].get(s, 0) >= best[s][1] for o in best):
                del best[s]
        for s, tk in best.items():
            queue[q].wait_ge(T.sem[s], tk[1])
            merge(known[q], tk[2])

    def note(q, tok, reads, writes):
        for name, lo, hi in writes:
            old = regs.get(name, [])
            regs[name] = [e for e in old if not (lo <= e[0] and e[1] <= hi)] + [(lo, hi, True, q, tok)]
        for name, lo, hi in reads:
            regs.setdefault(name, []).append((lo, hi, False, q, tok))

    def token(q, s, n):
        count[s] += n
        c = dict(known[q])
        merge(c, clocks[s])
        c[s] = count[s]
        clocks[s] = c
        return (s, count[s], c)

    def run(q, reads, writes, fn):
        need(q, deps(q, reads, writes))
        fn().then_inc(T.sem[csem[q]], 1)
        tok = token(q, csem[q], 1)
        note(q, tok, reads, writes)
        return tok

    def dmas(s, jobs):
        ds = [deps(q, r, w) for q, r, w, o, i in jobs]
        toks = []
        for (q, r, w, o, i), d in zip(jobs, ds):
            need(q, d)
            queue[q].dma_start(o, i).then_inc(T.sem[s], 16)
            toks.append(token(q, s, 16))
        for q, r, w, o, i in jobs:
            note(q, toks[-1], r, w)
        return toks[-1]

    def R(name, lo=0, hi=None):
        return (name, lo, 1 << 20 if hi is None else hi)

    def bank(j, n):
        return T.ps[:, 512 * j:512 * j + n]

    def mm(j, n, a, sa, alo, b, sb, blo, start, stop):
        run("t", [R(a, alo, alo + 128), R(sa, alo, alo + 128), R(b, blo, blo + n), R(sb, blo, blo + n)], [R("bank%d" % j)],
            lambda: g.tensor.matmul_mx(bank(j, n), T[a][:, alo:alo + 128], T[sa][:, alo:alo + 128], T[b][:, blo:blo + n], T[sb][:, blo:blo + n], start, stop))

    def vec(reads, writes, fn):
        return run("v", reads, writes, fn)

    def act(reads, writes, fn):
        return run("a", reads, writes, fn)

    def fill(name, view, c, lo=0, hi=None):
        vec([], [R(name, lo, hi)], lambda: g.vector.memset(view, c))

    def iota(name, view, pat, base, lo=0, hi=None):
        run("g", [], [R(name, lo, hi)], lambda: g.iota(view, pat, base, 0, allow_small_or_imprecise_dtypes=True))

    def quant(q, s, lo, n, tile, tlo, names):
        vec(names, [R(q, lo, lo + n), R(s, lo, lo + n)], lambda: g.vector.quantize_mx(T[q][:, lo:lo + n], T[s][:, lo:lo + n], T[tile][:, tlo:tlo + 4 * n]))

    def column(j, nm, sc, b):
        vec([R(nm)], [R("col", j, j + 1)], lambda: g.vector.tensor_scalar(T.col[:, j:j + 1], T[nm][:, 0:1], sc, b, ALU.mult, ALU.add))

    def bits(nm, m):
        vec([R("ip")], [R(nm)], lambda: g.vector.tensor_scalar(T[nm][:, 0:1], T.ip[:, 0:1], m, None, ALU.bitwise_and))

    xtok = dmas("ldx", [("s", [], [R("xin")], T.xin[:], T.x[:])])
    dmas("ldu", [("a", [], [R("uin")], T.uin[:], T.u[:])])

    fill("c32", T.c32[:], 32.0)
    run("g", [], [R("ip")], lambda: g.iota(T.ip[:, 0:1], [[0, 1]], 0, 1))
    run("g", [R("c32")], [R("dd")], lambda: g.affine_select(T.dd[:], T.c32[:], [[1, 516]], ALU.is_equal, 0.0, -3, -4))
    for blk, base, pat in ((0, 0, [[20, 2], [4, 4], [1, 2]]), (1, 2, [[20, 2], [4, 4], [1, 2]]), (2, 0, [[2, 2], [4, 4], [1, 2]])):
        for h in range(2):
            lo = 32 * blk + 16 * h
            iota("cz", T.cz[:, lo:lo + 16], pat, base, lo, lo + 16)
    iota("mones", T.mones[:], [[0, 256]], -1)
    iota("mone7", T.mone7[:], [[0, 8]], -1)
    iota("ones", T.ones[:], [[0, C]], 1)
    iota("zeros", T.zeros[:], [[0, C]], 0)
    iota("nb", T.nb[:], [[0, 32]], 0)
    iota("ot2", T.ot2[:], [[0, 32]], 0)
    iota("kf", T.kf[:], [[0, 64]], 0)
    fill("rst", T.rst[:], BIG)
    bits("t2", 16)
    bits("t1", 96)
    bits("t3", 31)
    column(3, "t2", -0.0625, 1.0)
    column(2, "t2", 0.0625, 0.0)
    column(0, "t1", 1.0, 16.0)
    column(1, "t1", 1.0, 32.0)
    column(4, "t3", 16.0, 16.0)
    act([R("dd"), R("col", 3, 4)], [R("dde")], lambda: g.scalar.activation(T.dde[:], T.dd[:], ACT.Copy, scale=T.col[:, 3:4]))
    act([R("dd"), R("col", 2, 3)], [R("ddo")], lambda: g.scalar.activation(T.ddo[:], T.dd[:], ACT.Copy, scale=T.col[:, 2:3]))
    fill("rst", T.rst[:, 0:128:16], -BIG)
    fill("pa", T.pa[:, 0:288:144], -BIG, 0, 1)
    fill("pb", T.pb[:, 0:8 * PS:PS], -BIG)
    fill("bigc", T.bigc[:], BIG)
    for b in range(4):
        quant("cf", "scf", 128 * b, 128, "dd", 3 - b, [R("dd")])
    for b in range(4):
        quant("ce", "sce", 128 * b, 128, "dde", 3 - b, [R("dde")])
    quant("qu", "squ", 0, 128, "uin", 0, [R("uin")])
    for b in range(4):
        quant("cd", "scd", 128 * b, 128, "ddo", 3 - b, [R("ddo")])
    quant("qx0", "sx0", 0, C, "xin", 0, [R("xin")])
    need("s", [xtok])
    dmas("ldw", [("s", [], [R("wq")], T.wq[:].bitcast(dt.uint8), T.wc[:])])
    dmas("ldp", [("s", [], [R("wsc")], T.wsc[:], T.ws[:])])
    dmas("ldv", [("s", [], [R("vin")], T.vin[:], T.v[:])])

    SB, SB2, YB = 6, 7, 7
    RB = [4, 5, 0, 1]
    VB = [2, 3, 4, 5]
    ncol = [16 * (k % 2) + k // 2 for k in range(8)]
    for r in range(3):
        last = r == 2
        X, SX, X1, SX1 = "qx%d" % r, "sx%d" % r, "qx%d" % (r + 1), "sx%d" % (r + 1)
        U, SU = ("qu", "squ") if r == 0 else ("land%d" % r, "lsc%d" % r)
        ue, se, uo, so, qz, sz, pk, sk, qv, sv = [n + str(r) for n in ("ue", "se", "uo", "so", "qz", "sz", "pk", "sk", "qv", "sv")]

        def tee(b, j):
            mm(j, C, "cf", "scf", 128 * b, X, SX, 0, True, False)

        if r:
            for b in range(4):
                tee(b, b)
        for h in range(2):
            mm(4 + h, 128, X, SX, 96 * h, U, SU, 0, True, True)
        mm(SB, C, U, SU, 0, X, SX, 0, True, True)
        mm(SB2, C, U, SU, 0, X, SX, 0, True, True)
        if not r:
            for b in range(4):
                tee(b, b)
        for h in range(2):
            p0 = 144 * h
            vec([R("bank%d" % (4 + h)), R("rst")], [R("pa", p0 + 1, p0 + 129)],
                lambda: g.vector.tensor_tensor_scan(T.pa[:, p0 + 1:p0 + 129], T.rst[:], bank(4 + h, 128), -BIG, ALU.min, ALU.max))
        for h in range(2):
            p0 = 144 * h
            vec([R("bank%d" % (4 + h)), R("pa", p0, p0 + 128)], [R("nr", 128 * h, 128 * h + 128)],
                lambda: g.vector.tensor_tensor(T.nr[:, 128 * h:128 * h + 128], bank(4 + h, 128), T.pa[:, p0:p0 + 128], ALU.is_le))
        for b in range(2):
            tee(b, RB[b])
        vec([R("nr"), R("mones")], [R("ag")], lambda: g.vector.tensor_tensor_scan(T.ag[:], T.nr[:], T.mones[:], 0.0, ALU.mult, ALU.add))
        if not r:
            vec([R("cz")], [R("czt")], lambda: g.vector.transpose(T.czt[:], T.cz[:]))
        vec([R("ag")], [R("kt")], lambda: g.vector.transpose(T.kt[:], T.ag[:]))
        dmas("dk", [("s" if h == 0 else "a", [R("kt")], [R("ot", 0, 16)], T.ot[32 * a + 16 * h:32 * a + 16 * h + 16, 0:16],
                     T.kt[15:128:16, 128 * h + 32 * a:128 * h + 32 * a + 32]) for a in range(4) for h in range(2)])
        if not r:
            vec([R("czt")], [R("off")], lambda: g.vector.tensor_scalar(T.off[:, 0:6:2], T.czt[:, 0:96:32], 31.0, None, ALU.min))

        def scan(k):
            o = PS * k
            d1 = [R("bigc")] if k == 0 else [R("pb", o - PS, o - PS + 224)]
            vec([R("bank%d" % SB)] + d1, [R("pb", o + 1, o + 225)],
                lambda: g.vector.tensor_tensor_scan(T.pb[:, o + 1:o + 225], bank(SB, C), T.bigc[:] if k == 0 else T.pb[:, o - PS:o - PS + 224], -BIG, ALU.max, ALU.min))

        def sign(k):
            o = PS * k + 224
            act([R("bank%d" % SB2), R("pb", o, o + 1)], [R("sg", C * k, C * k + C)],
                lambda: g.scalar.activation(T.sg[:, C * k:C * k + C], bank(SB2, C), ACT.Sign, bias=T.pb[:, o:o + 1], scale=-1.0))

        def flags(k):
            o = PS * k + 224
            if k in NS:
                vec([R("sg", C * k, C * k + C)], [R("fb", C * k, C * k + C)],
                    lambda: g.vector.tensor_scalar(T.fb[:, C * k:C * k + C], T.sg[:, C * k:C * k + C], 0.0, None, ALU.is_equal))
            else:
                vec([R("bank%d" % SB), R("pb", o, o + 1)], [R("fb", C * k, C * k + C)],
                    lambda: g.vector.tensor_scalar(T.fb[:, C * k:C * k + C], bank(SB, C), T.pb[:, o:o + 1], None, ALU.is_equal))

        def same(k):
            vec([R("pb")], [R("eq")], lambda: g.vector.tensor_tensor(T.eq[:, 1:8], T.pb[:, PS + 224:8 * PS:PS], T.pb[:, 224:7 * PS:PS], ALU.is_equal))

        def less(k):
            vec([R("eq"), R("mone7")], [R("ne")], lambda: g.vector.tensor_tensor_scan(T.ne[:, 1:8], T.mone7[:, 0:7], T.eq[:, 1:8], 0.0, ALU.add, ALU.mult))

        def counts(k):
            vec([R("fb", C * k, C * k + C), R("ne"), R("ones")], [R("cb", C * k, C * k + C)],
                lambda: g.vector.tensor_tensor_scan(T.cb[:, C * k:C * k + C], T.fb[:, C * k:C * k + C], T.ones[:], T.ne[:, k:k + 1], ALU.add, ALU.min))

        def places(k):
            if k == 0:
                act([R("pb", 0, 225)], [R("nb", ncol[0], ncol[0] + 1), R("junk", 0, C)],
                    lambda: g.scalar.activation(T.junk[:, 0:C], T.pb[:, 1:225], ACT.Sign, bias=T.pb[:, 224:225], scale=-1.0, accum_out=T.nb[:, ncol[0]:ncol[0] + 1]))
            else:
                act([R("cb", C * k, C * k + C)], [R("nb", ncol[k], ncol[k] + 1), R("junk", C * k, C * k + C)],
                    lambda: g.scalar.activation(T.junk[:, C * k:C * k + C], T.cb[:, C * k:C * k + C], ACT.Sign, bias=1.0, scale=-1.0, accum_out=T.nb[:, ncol[k]:ncol[k] + 1]))

        def rest(k):
            vec([R("cb", C * k, C * k + C), R("zeros")], [R("junk", C * k, C * k + C)],
                lambda: g.vector.tensor_tensor_scan(T.junk[:, C * k:C * k + C], T.cb[:, C * k:C * k + C], T.zeros[:], 0.0, ALU.add, ALU.max))

        def pair(k):
            vec([R("junk", C * k, C * k + 2 * C)], [R("nb", ncol[k], ncol[k] + 1), R("nb", ncol[k + 1], ncol[k + 1] + 1)],
                lambda: g.vector.tensor_scalar(T.nb[:, ncol[k]:ncol[k + 1] + 1:16], T.junk[:, C * k + C - 1:C * k + 2 * C:C], -1.0, float(C), ALU.mult, ALU.add))

        def halves(k):
            vec([R("ot", 0, 16)], [R("ot", 16, 32)], lambda: g.vector.tensor_copy(T.ot[:, 16:32], T.ot[:, 0:16]))

        def turn(k):
            vec([R("ot")], [R("ott")], lambda: g.vector.transpose(T.ott[:], T.ot[:]))

        def picks(e):
            q, s = ((ue, se), (uo, so))[e]
            vec([R("ott"), R("off"), R("col")], [R("lst", 16 * e, 16 * e + 16)],
                lambda: g.vector.tensor_scalar(T.lst[:, 16 * e:16 * e + 16], T.ott[:, 0:32].indirect(T.off[:, 2 * e:2 * e + 1]), -16.0, T.col[:, e:e + 1], ALU.max, ALU.add))
            vec([R(U), R("lst", 16 * e, 16 * e + 16)], [R(q)],
                lambda: g.vector.tensor_copy(T[q][:].bitcast(dt.uint32), T[U][:].bitcast(dt.uint32).indirect(T.lst[:, 16 * e:16 * e + 14])))
            act([R(SU), R("lst", 16 * e, 16 * e + 16)], [R(s)],
                lambda: g.scalar.activation(T[s][:], T[SU][:].indirect(T.lst[:, 16 * e:16 * e + 14]), ACT.Copy))
            for b in range(4):
                mm(b, C, ("ce", "cd")[e], ("sce", "scd")[e], 128 * b, q, s, 0, False, e == 1)

        def zed(b):
            act([R("bank%d" % b)], [R("zt%d" % b)], lambda: g.scalar.activation(T.zt[:, b:4 * C:4], bank(b, C), ACT.Copy, scale=2.0 ** -6))

        def zedv(b):
            vec([R("bank%d" % b)], [R("zt%d" % b)], lambda: g.vector.tensor_scalar(T.zt[:, b:4 * C:4], bank(b, C), 2.0 ** -6, None, ALU.mult))

        def send_lists(k):
            vec([R("nb")], [R("nt")], lambda: g.vector.transpose(T.nt[:], T.nb[:]))
            dmas("dn", [("sa"[h], [R("nt")], [R("ot2", 16 * h, 16 * h + 16)], T.ot2[32 * a:32 * a + 16, 16 * h:16 * h + 16], T.nt[a:128:16, 0:32])
                        for a in range(4) for h in range(2)])

        def state(k):
            for b in (2, 3):
                tee(b, RB[b])
            quant(qz, sz, 0, C, "zt", 0, [R("zt%d" % b) for b in range(4)])
            for b in range(4):
                mm(RB[b], C, "wq", "wsc", 128 * b, qz, sz, 0, False, True)

        def newx(b):
            act([R("bank%d" % RB[b])], [R("xt%d" % b)], lambda: g.scalar.activation(T.xt[:, b:4 * C:4], bank(RB[b], C), ACT.Copy, scale=2.0 ** -5))

        def newxv(b):
            vec([R("bank%d" % RB[b])], [R("xt%d" % b)], lambda: g.vector.tensor_scalar(T.xt[:, b:4 * C:4], bank(RB[b], C), 2.0 ** -5, None, ALU.mult))

        steps = {"s": scan, "n": sign, "f": flags, "q": same, "e": less, "c": counts, "p": places, "w": rest, "P": pair,
                 "D": halves, "X": turn, "E": lambda k: picks(0), "O": lambda k: picks(1), "Z": zed, "z": zedv,
                 "N": send_lists, "Q": state, "R": newx, "r": newxv}
        for word in SEQ.split():
            steps[word[0]](int(word[1:] or "0"))
        quant(X1, SX1, 0, C, "xt", 0, [R("xt%d" % b) for b in range(4)])
        vec([R("ot2")], [R("ott2")], lambda: g.vector.transpose(T.ott2[:], T.ot2[:]))
        vec([R("ott2"), R("off")], [R("lst2")], lambda: g.vector.tensor_copy(T.lst2[:], T.ott2[:, 0:32].indirect(T.off[:, 4:5])))
        for e in range(2):
            lo = 128 * e
            vec([R(X1), R("lst2")], [R(pk, lo, lo + 128)],
                lambda: g.vector.tensor_copy(T[pk][:, lo:lo + 128].bitcast(dt.uint32), T[X1][:].bitcast(dt.uint32).indirect(T.lst2[:, 8 * e:8 * e + 8])))
            act([R(SX1), R("lst2")], [R(sk, lo, lo + 128)],
                lambda: g.scalar.activation(T[sk][:, lo:lo + 128], T[SX1][:].indirect(T.lst2[:, 8 * e:8 * e + 8]), ACT.Copy))
            for b in range(4):
                mm(VB[b], 128, ("ce", "cd")[e], ("sce", "scd")[e], 128 * b, pk, sk, lo, e == 0, e == 1)
        for b in range(4):
            if b % 2 == 0:
                act([R("bank%d" % VB[b])], [R("vt%d" % b)], lambda: g.scalar.activation(T.vt[:, b:512:4], bank(VB[b], 128), ACT.Copy, scale=2.0 ** -5))
            else:
                vec([R("bank%d" % VB[b])], [R("vt%d" % b)], lambda: g.vector.tensor_scalar(T.vt[:, b:512:4], bank(VB[b], 128), 2.0 ** -5, None, ALU.mult))
        quant(qv, sv, 0, 128, "vt", 0, [R("vt%d" % b) for b in range(4)])
        dst = T.cores[(rank + STEP[r]) % 8]
        src = T.cores[(rank - STEP[r]) % 8]
        rid, pid = topo.addr(dst, core)
        need("g", deps("g", [R(qv), R(sv)], []))
        arr = "arr%d" % (r + 1)
        ld, ls = T["land%d" % (r + 1)], T["lsc%d" % (r + 1)]
        g.remote_dma(ld[:].bitcast(dt.uint8), T[qv][:].bitcast(dt.uint8), T.sem[arr], T.sem["loc"], pid, rid, topo.mask(core, dst))
        g.remote_dma(ls[:], T[sv][:], T.sem[arr], T.sem["loc"], pid, rid, topo.mask(core, dst))
        count["loc"] += 2 * len(topo.engines(core, dst))
        count[arr] = 2 * len(topo.engines(src, core))
        note("g", (arr, count[arr], {arr: count[arr]}), [], [R("land%d" % (r + 1)), R("lsc%d" % (r + 1))])
        if r == 0:
            quant("qvv", "sqvv", 0, 128, "vin", 0, [R("vin")])
    for h in range(2):
        vec([R("ag")], [R("kf", 32 * h, 32 * h + 8)], lambda: g.vector.tensor_copy(T.kf[:, 32 * h:32 * h + 8], T.ag[:, 128 * h + 15:128 * h + 128:16]))
    vec([R("kf")], [R("kft")], lambda: g.vector.transpose(T.kft[:], T.kf[:]))
    vec([R("kft"), R("col")], [R("kfo")], lambda: g.vector.tensor_scalar(T.kfo[:], T.kft[:], -16.0, T.col[:, 4:5], ALU.max, ALU.add))
    mm(YB, C, "qvv", "sqvv", 0, "qx3", "sx3", 0, True, True)
    act([R("bank%d" % YB)], [R("yb")], lambda: g.scalar.activation(T.yb[:], bank(YB, C), ACT.Copy))
    jobs = [("s", [R("qx3")], [], T.oc[:], T.qx3[:].bitcast(dt.uint8))]
    jobs += [("s", [R("sx3")], [], T.osc[4 * k:4 * k + 4, :], T.sx3[32 * k:32 * k + 4, :]) for k in range(4)]
    for A in range(4):
        for e in range(2):
            jobs.append(("s", [R("nt")], [], T.op[e:8:2, 224 + 32 * A:256 + 32 * A], T.nt[32 * A + 16 * e:32 * A + 16 * e + 4, 0:32]))
    jobs.append(("s", [R("yb")], [], T.y[:], T.yb[:]))
    for A in range(4):
        for h in range(2):
            if h == 0 or A:
                jobs.append(("s", [R("kfo")], [], T.op[0:8, 96 * h + 32 * A:96 * h + 32 * A + 32], T.kfo[32 * A:32 * A + 8, 32 * h:32 * h + 32]))
    dmas("st", jobs)
    jobs = [("s", [R("land3")], [], T.uc[:], T.land3[:].bitcast(dt.uint8))]
    jobs += [("as"[k % 2], [R("lsc3")], [], T.usc[4 * k:4 * k + 4, :], T.lsc3[32 * k:32 * k + 4, :]) for k in range(4)]
    dmas("st", jobs)
    g.wait_ge(T.sem["loc"], count["loc"])
    for s in ("vs", "ts", "sa", "gc0", "dk", "dn", "ldx", "ldu", "ldv", "ldw", "ldp", "st"):
        g.sync.wait_ge(T.sem[s], count[s])
